import numpy as np, ml_dtypes
CORES = [14,30,46,142,158,174,270,286,302,398,414,430]
N = 12
TK = 128
WID = [48,80,16,112,16,32,16,80,16,112,128,112]
def setup_inputs(rng):
    return {"x": rng.standard_normal((N, 128, TK), dtype=np.float32).astype(ml_dtypes.bfloat16), "w1": (rng.standard_normal((N, 128, 128), dtype=np.float32) / 8).astype(ml_dtypes.bfloat16), "w2": (rng.standard_normal((N, 128, 128), dtype=np.float32) / 8).astype(ml_dtypes.bfloat16)}
def setup_inputs_big(rng):
    d = setup_inputs(rng)
    for k in ("x", "w1", "w2"): d[k] = (d[k].astype(np.float32) * 1024.0).astype(d[k].dtype)
    return d
def setup_inputs_small(rng):
    d = setup_inputs(rng)
    for k in ("x", "w1", "w2"): d[k] = (d[k].astype(np.float32) * (1 / 1024.0)).astype(d[k].dtype)
    return d
def setup_inputs_apart(rng):
    d = setup_inputs(rng)
    f = (10.0 ** rng.permutation(np.linspace(-1.5, 1.5, N))).astype(np.float32).reshape(N, 1, 1)
    for k in ("x", "w1", "w2"): d[k] = (d[k].astype(np.float32) * f).astype(d[k].dtype)
    return d
def whole(x, w1, w2):
    X, W1, W2 = x.astype(np.float64), w1.astype(np.float64), w2.astype(np.float64)
    y = np.zeros((N, 128, TK))
    for r in range(N):
        for j in range(N):
            y[r] += W2[j].T @ np.maximum(W1[j].T @ X[r], 0.0)
    return {"y": y.astype(ml_dtypes.bfloat16 if x.dtype != np.float64 else np.float64)}
def reference(x, w1, w2):
    o = whole(x, w1, w2)["y"].copy()
    for r in range(N):
        o[r][:, WID[r]:] = np.nan
    return {"y": o}

@@ -1,0 +1,141 @@
+from concourse.bass import DstId, RemoteDMATransfer
+from concourse.mybir import AluOpType
+
+XW = 352
+
+SCRATCH = {
+    "xs": ("sbuf", [128, XW], "bfloat16"),
+    "w_own": ("sbuf", [128, 256], "bfloat16"),
+    "w_far": ("sbuf", [128, 256], "bfloat16"),
+    "w_near": ("sbuf", [128, 256], "bfloat16"),
+    "w_diag": ("sbuf", [128, 256], "bfloat16"),
+    "h0": ("sbuf", [128, XW], "bfloat16"),
+    "h1": ("sbuf", [128, XW], "bfloat16"),
+    "h2": ("sbuf", [128, XW], "bfloat16"),
+    "h3": ("sbuf", [128, XW], "bfloat16"),
+    "zero": ("sbuf", [128, XW], "bfloat16"),
+    "pout": ("sbuf", [128, 256], "bfloat16"),
+    "pin0": ("sbuf", [128, 128], "bfloat16"),
+    "pin1": ("sbuf", [128, 128], "bfloat16"),
+    "ysb": ("sbuf", [128, 128], "bfloat16"),
+    "hp0": ("psum", [128, 512], "float32"),
+    "hp1": ("psum", [128, 512], "float32"),
+    "hp2": ("psum", [128, 512], "float32"),
+    "hp3": ("psum", [128, 512], "float32"),
+    "hp4": ("psum", [128, 512], "float32"),
+    "yp": ("psum", [128, 512], "float32"),
+    "ys": ("psum", [128, 512], "float32"),
+    "t1": ("psum", [128, 512], "float32"),
+}
+SEMAPHORES = ["ldw", "ldx", "sent", "a_far", "a_near", "a_diag", "a_x", "a_p0", "a_p1", "fill", "pe", "ve", "st"]
+
+
+def _engines(mask):
+    return bin(mask).count("1")
+
+
+def _row(c, cores, topo):
+    row = [d for d in cores if topo.host(d) == topo.host(c)]
+    i = row.index(c)
+    return row[i + 1:] + row[:i] + [c]
+
+
+def rank_program(g, core, T, topo):
+    rank = T.rank_of(core)
+    if rank is None:
+        return
+    cores, S = list(T.cores), T.sem
+    wid = {d: T.tables["WID"][T.rank_of(d)] for d in cores}
+    te, ve = g.tensor, g.vector
+
+    col = [d for d in cores if d != core and topo.chip(d) == topo.chip(core)]
+    my_rack = topo.rack(topo.host(core))
+    near = [d for d in col if topo.rack(topo.host(d)) == my_rack][0]
+    far = [d for d in col if topo.rack(topo.host(d)) != my_rack and topo.may_write(core, d)][0]
+
+    def offset(holder, src):
+        o = 0
+        for d in _row(holder, cores, topo):
+            if d == src:
+                return o
+            o += wid[d]
+
+    nxt, prv = _row(core, cores, topo)[:2]
+    wp, ws = wid[nxt] + wid[prv], wid[core]
+    wt = wp + ws
+    sent = [0]
+
+    def write(dst, out_ap, in_ap, sem):
+        rid, pid = topo.addr(dst, core)
+        m = topo.mask(core, dst)
+        g.remote_dma(out_ap=out_ap, in_ap=in_ap, remote_sem=sem, local_sem=S.sent, pid=pid, routing_id=rid,
+                     dma_engine_mask=m)
+        sent[0] += _engines(m)
+        return _engines(m)
+
+    g.sync.dma_start(T.w_own[:, 0:128], T.w1[:, :]).then_inc(S.ldw, 16)
+    g.scalar.dma_start(T.w_own[:, 128:256], T.w2[:, :]).then_inc(S.ldw, 16)
+    g.sync.dma_start(T.xs[:, wp:wt], T.x[:, 0:ws]).then_inc(S.ldx, 16)
+    ve.memset(T.zero[:, 0:wt], 0.0).then_inc(S.fill, 1)
+
+    g.wait_ge(S.ldw, 32)
+    n8 = write(far, T.w_far[:], T.w_own[:], S.a_far)
+    g.wait_ge(S.ldx, 16)
+    m = topo.mask(core, nxt) & topo.mask(core, prv)
+    ids = [topo.addr(d, core) for d in (nxt, prv)]
+    g.remote_dma_fused([RemoteDMATransfer(
+        dst_ids=[DstId(rid=r, pnc=p) for r, p in ids], dma_engine_mask=m, remote_sem=S.a_x,
+        srcs=[T.xs[:, wp:wt]],
+        dsts=[T.xs[:, offset(d, core):offset(d, core) + ws] for d in (nxt, prv)], alu_op=0)], local_sem=S.sent)
+    sent[0] += _engines(m)
+    nx = 2 * _engines(m)
+    write(near, T.w_near[:], T.w_own[:], S.a_near)
+    g.wait_ge(S.a_far, n8)
+    write(near, T.w_diag[:], T.w_far[:], S.a_diag)
+    g.wait_ge(S.ve, 5)
+    write(nxt, T.pin0[:, 0:wid[nxt]], T.pout[:, 0:wid[nxt]], S.a_p0)
+    write(prv, T.pin1[:, 0:wid[prv]], T.pout[:, wid[nxt]:wp], S.a_p1)
+    g.wait_ge(S.sent, sent[0])
+
+    tiles = [(T.w_own, None), (T.w_far, S.a_far), (T.w_near, S.a_near), (T.w_diag, S.a_diag)]
+    hs = [T.h0, T.h1, T.h2, T.h3]
+    hp = [T.hp0, T.hp1, T.hp2]
+    te.wait_ge(S.ldw, 32)
+    te.wait_ge(S.ldx, 16)
+    te.wait_ge(S.a_x, nx)
+    for i in range(3):
+        w, sem = tiles[i]
+        if sem is not None:
+            te.wait_ge(sem, n8)
+        te.matmul(hp[i][:, 0:wt], w[:, 0:128], T.xs[:, 0:wt], start=True, stop=True).then_inc(S.pe, 1)
+        te.wait_ge(S.ve, i + 1)
+        te.matmul(T.yp[:, 0:wp], w[:, 128:256], hs[i][:, 0:wp], start=(i == 0), stop=False)
+        te.matmul(T.ys[:, 0:ws], w[:, 128:256], hs[i][:, wp:wt], start=(i == 0), stop=False)
+    w = T.w_diag
+    te.wait_ge(S.a_diag, n8)
+    te.matmul(T.hp3[:, 0:wp], w[:, 0:128], T.xs[:, 0:wp], start=True, stop=True).then_inc(S.pe, 1)
+    te.matmul(T.hp4[:, 0:ws], w[:, 0:128], T.xs[:, wp:wt], start=True, stop=True).then_inc(S.pe, 1)
+    te.wait_ge(S.ve, 4)
+    te.matmul(T.yp[:, 0:wp], w[:, 128:256], T.h3[:, 0:wp], start=False, stop=True).then_inc(S.pe, 1)
+    te.wait_ge(S.ve, 6)
+    te.matmul(T.ys[:, 0:ws], w[:, 128:256], T.h3[:, wp:wt], start=False, stop=True).then_inc(S.pe, 1)
+
+    ve.wait_ge(S.fill, 1)
+    for i in range(3):
+        ve.wait_ge(S.pe, i + 1)
+        ve.tensor_tensor(hs[i][:, 0:wt], hp[i][:, 0:wt], T.zero[:, 0:wt], op=AluOpType.max).then_inc(S.ve, 1)
+    ve.wait_ge(S.pe, 4)
+    ve.tensor_tensor(T.h3[:, 0:wp], T.hp3[:, 0:wp], T.zero[:, 0:wp], op=AluOpType.max).then_inc(S.ve, 1)
+    ve.wait_ge(S.pe, 6)
+    ve.tensor_copy(T.pout[:, 0:wp], T.yp[:, 0:wp]).then_inc(S.ve, 1)
+    ve.tensor_tensor(T.h3[:, wp:wt], T.hp4[:, 0:ws], T.zero[:, 0:ws], op=AluOpType.max).then_inc(S.ve, 1)
+    ve.wait_ge(S.pe, 7)
+    ve.wait_ge(S.a_p0, n8)
+    ve.tensor_tensor(T.t1[:, 0:ws], T.ys[:, 0:ws], T.pin0[:, 0:ws], op=AluOpType.add).then_inc(S.ve, 1)
+    ve.wait_ge(S.ve, 7)
+    ve.wait_ge(S.a_p1, n8)
+    ve.tensor_tensor(T.ysb[:, 0:ws], T.t1[:, 0:ws], T.pin1[:, 0:ws], op=AluOpType.add).then_inc(S.ve, 1)
+
+    g.sync.wait_ge(S.ve, 8)
+    g.sync.dma_start(T.y[:, 0:ws], T.ysb[:, 0:ws]).then_inc(S.st, 16)
+    g.sync.wait_ge(S.st, 16)

@@ -1,18 +1,22 @@
 from concourse.bass import DstId, RemoteDMATransfer
 from concourse.mybir import AluOpType
 
-XW = 352
+XW = 304
 
 SCRATCH = {
     "xs": ("sbuf", [128, XW], "bfloat16"),
     "w_own": ("sbuf", [128, 256], "bfloat16"),
     "w_far": ("sbuf", [128, 256], "bfloat16"),
     "w_near": ("sbuf", [128, 256], "bfloat16"),
-    "w_diag": ("sbuf", [128, 256], "bfloat16"),
+    "w_d0": ("sbuf", [128, 256], "bfloat16"),
+    "w_d1": ("sbuf", [128, 256], "bfloat16"),
+    "w_d2": ("sbuf", [128, 256], "bfloat16"),
     "h0": ("sbuf", [128, XW], "bfloat16"),
     "h1": ("sbuf", [128, XW], "bfloat16"),
     "h2": ("sbuf", [128, XW], "bfloat16"),
-    "h3": ("sbuf", [128, XW], "bfloat16"),
+    "hd0": ("sbuf", [128, 128], "bfloat16"),
+    "hd1": ("sbuf", [128, 128], "bfloat16"),
+    "hd2": ("sbuf", [128, 128], "bfloat16"),
     "zero": ("sbuf", [128, XW], "bfloat16"),
     "pout": ("sbuf", [128, 256], "bfloat16"),
     "pin0": ("sbuf", [128, 128], "bfloat16"),
@@ -22,12 +26,12 @@ SCRATCH = {
     "hp1": ("psum", [128, 512], "float32"),
     "hp2": ("psum", [128, 512], "float32"),
     "hp3": ("psum", [128, 512], "float32"),
-    "hp4": ("psum", [128, 512], "float32"),
     "yp": ("psum", [128, 512], "float32"),
     "ys": ("psum", [128, 512], "float32"),
     "t1": ("psum", [128, 512], "float32"),
 }
-SEMAPHORES = ["ldw", "ldx", "sent", "a_far", "a_near", "a_diag", "a_x", "a_p0", "a_p1", "fill", "pe", "ve", "st"]
+SEMAPHORES = ["ldw", "ldx", "sent", "a_far", "a_near", "a_d0", "a_d1", "a_d2", "a_x", "a_p0", "a_p1", "fill", "pe",
+              "ve", "st"]
 
 
 def _engines(mask):
@@ -40,6 +44,15 @@ def _row(c, cores, topo):
     return row[i + 1:] + row[:i] + [c]
 
 
+def _near(c, cores, topo):
+    return [d for d in cores if d != c and topo.chip(d) == topo.chip(c)
+            and topo.rack(topo.host(d)) == topo.rack(topo.host(c))][0]
+
+
+def _visitors(c, cores, topo):
+    return _row(_near(c, cores, topo), cores, topo)[:-1]
+
+
 def rank_program(g, core, T, topo):
     rank = T.rank_of(core)
     if rank is None:
@@ -48,28 +61,33 @@ def rank_program(g, core, T, topo):
     wid = {d: T.tables["WID"][T.rank_of(d)] for d in cores}
     te, ve = g.tensor, g.vector
 
-    col = [d for d in cores if d != core and topo.chip(d) == topo.chip(core)]
-    my_rack = topo.rack(topo.host(core))
-    near = [d for d in col if topo.rack(topo.host(d)) == my_rack][0]
-    far = [d for d in col if topo.rack(topo.host(d)) != my_rack and topo.may_write(core, d)][0]
+    near = _near(core, cores, topo)
+    far = [d for d in cores if topo.chip(d) == topo.chip(core) and topo.rack(topo.host(d)) != topo.rack(topo.host(core))
+           and topo.may_write(core, d)][0]
+    chips = sorted({topo.chip(d) for d in cores})
+    place = chips.index(topo.chip(core))
+    nch = len(chips)
 
     def offset(holder, src):
         o = 0
-        for d in _row(holder, cores, topo):
+        for d in _visitors(holder, cores, topo):
             if d == src:
                 return o
             o += wid[d]
 
-    nxt, prv = _row(core, cores, topo)[:2]
-    wp, ws = wid[nxt] + wid[prv], wid[core]
+    v0, v1 = _visitors(core, cores, topo)
+    w0, wp, ws = wid[v0], wid[v0] + wid[v1], wid[core]
     wt = wp + ws
     sent = [0]
 
-    def write(dst, out_ap, in_ap, sem):
-        rid, pid = topo.addr(dst, core)
-        m = topo.mask(core, dst)
-        g.remote_dma(out_ap=out_ap, in_ap=in_ap, remote_sem=sem, local_sem=S.sent, pid=pid, routing_id=rid,
-                     dma_engine_mask=m)
+    def write(dsts, out_aps, in_ap, sem):
+        m = topo.mask(core, dsts[0])
+        for d in dsts:
+            m &= topo.mask(core, d)
+        ids = [topo.addr(d, core) for d in dsts]
+        g.remote_dma_fused([RemoteDMATransfer(
+            dst_ids=[DstId(rid=r, pnc=p) for r, p in ids], dma_engine_mask=m, remote_sem=sem,
+            srcs=[in_ap], dsts=out_aps, alu_op=0)], local_sem=S.sent)
         sent[0] += _engines(m)
         return _engines(m)
 
@@ -79,63 +97,73 @@ def rank_program(g, core, T, topo):
     ve.memset(T.zero[:, 0:wt], 0.0).then_inc(S.fill, 1)
 
     g.wait_ge(S.ldw, 32)
-    n8 = write(far, T.w_far[:], T.w_own[:], S.a_far)
+    n8 = write([far], [T.w_far[:]], T.w_own[:], S.a_far)
     g.wait_ge(S.ldx, 16)
-    m = topo.mask(core, nxt) & topo.mask(core, prv)
-    ids = [topo.addr(d, core) for d in (nxt, prv)]
-    g.remote_dma_fused([RemoteDMATransfer(
-        dst_ids=[DstId(rid=r, pnc=p) for r, p in ids], dma_engine_mask=m, remote_sem=S.a_x,
-        srcs=[T.xs[:, wp:wt]],
-        dsts=[T.xs[:, offset(d, core):offset(d, core) + ws] for d in (nxt, prv)], alu_op=0)], local_sem=S.sent)
-    sent[0] += _engines(m)
-    nx = 2 * _engines(m)
-    write(near, T.w_near[:], T.w_own[:], S.a_near)
+    write([v0, v1], [T.xs[:, offset(d, core):offset(d, core) + ws] for d in (v0, v1)], T.xs[:, wp:wt], S.a_x)
+    write([near], [T.w_near[:]], T.w_own[:], S.a_near)
+    there = [near] + _row(core, cores, topo)[:-1]
     g.wait_ge(S.a_far, n8)
-    write(near, T.w_diag[:], T.w_far[:], S.a_diag)
+    write(there, [T["w_d%d" % place][:] for d in there], T.w_far[:], S["a_d%d" % place])
+    g.wait_ge(S.ve, 4)
+    write([v0], [T.pin0[:, 0:w0]], T.pout[:, 0:w0], S.a_p0)
     g.wait_ge(S.ve, 5)
-    write(nxt, T.pin0[:, 0:wid[nxt]], T.pout[:, 0:wid[nxt]], S.a_p0)
-    write(prv, T.pin1[:, 0:wid[prv]], T.pout[:, wid[nxt]:wp], S.a_p1)
+    write([v1], [T.pin1[:, 0:wp - w0]], T.pout[:, w0:wp], S.a_p1)
     g.wait_ge(S.sent, sent[0])
 
-    tiles = [(T.w_own, None), (T.w_far, S.a_far), (T.w_near, S.a_near), (T.w_diag, S.a_diag)]
-    hs = [T.h0, T.h1, T.h2, T.h3]
-    hp = [T.hp0, T.hp1, T.hp2]
+    relu = AluOpType.max
     te.wait_ge(S.ldw, 32)
     te.wait_ge(S.ldx, 16)
-    te.wait_ge(S.a_x, nx)
-    for i in range(3):
-        w, sem = tiles[i]
-        if sem is not None:
-            te.wait_ge(sem, n8)
-        te.matmul(hp[i][:, 0:wt], w[:, 0:128], T.xs[:, 0:wt], start=True, stop=True).then_inc(S.pe, 1)
-        te.wait_ge(S.ve, i + 1)
-        te.matmul(T.yp[:, 0:wp], w[:, 128:256], hs[i][:, 0:wp], start=(i == 0), stop=False)
-        te.matmul(T.ys[:, 0:ws], w[:, 128:256], hs[i][:, wp:wt], start=(i == 0), stop=False)
-    w = T.w_diag
-    te.wait_ge(S.a_diag, n8)
-    te.matmul(T.hp3[:, 0:wp], w[:, 0:128], T.xs[:, 0:wp], start=True, stop=True).then_inc(S.pe, 1)
-    te.matmul(T.hp4[:, 0:ws], w[:, 0:128], T.xs[:, wp:wt], start=True, stop=True).then_inc(S.pe, 1)
-    te.wait_ge(S.ve, 4)
-    te.matmul(T.yp[:, 0:wp], w[:, 128:256], T.h3[:, 0:wp], start=False, stop=True).then_inc(S.pe, 1)
+    te.wait_ge(S.a_x, 2 * n8)
+    w = T.w_own
+    te.matmul(T.hp0[:, 0:wt], w[:, 0:128], T.xs[:, 0:wt], start=True, stop=True).then_inc(S.pe, 1)
+    te.wait_ge(S.ve, 1)
+    te.matmul(T.yp[:, 0:wp], w[:, 128:256], T.h0[:, 0:wp], start=True, stop=False)
+    te.matmul(T.ys[:, 0:ws], w[:, 128:256], T.h0[:, wp:wt], start=True, stop=False)
+    w = T.w_far
+    te.wait_ge(S.a_far, n8)
+    te.matmul(T.hp1[:, 0:wt], w[:, 0:128], T.xs[:, 0:wt], start=True, stop=True).then_inc(S.pe, 1)
+    te.wait_ge(S.ve, 2)
+    te.matmul(T.yp[:, 0:wp], w[:, 128:256], T.h1[:, 0:wp], start=False, stop=False)
+    te.matmul(T.ys[:, 0:ws], w[:, 128:256], T.h1[:, wp:wt], start=False, stop=False)
+    w = T.w_near
+    te.wait_ge(S.a_near, n8)
+    te.matmul(T.hp2[:, 0:wp], w[:, 0:128], T.xs[:, 0:wp], start=True, stop=True).then_inc(S.pe, 1)
+    te.matmul(T.hp3[:, 0:ws], w[:, 0:128], T.xs[:, wp:wt], start=True, stop=True).then_inc(S.pe, 1)
+    te.wait_ge(S.ve, 3)
+    te.matmul(T.yp[:, 0:wp], w[:, 128:256], T.h2[:, 0:wp], start=False, stop=True).then_inc(S.pe, 1)
     te.wait_ge(S.ve, 6)
-    te.matmul(T.ys[:, 0:ws], w[:, 128:256], T.h3[:, wp:wt], start=False, stop=True).then_inc(S.pe, 1)
+    te.matmul(T.ys[:, 0:ws], w[:, 128:256], T.h2[:, wp:wt], start=False, stop=False)
+    order = [(place - k) % nch for k in range(nch)]
+    hpd = [T.hp0, T.hp1, T.hp2]
+    for k, j in enumerate(order):
+        w = T["w_d%d" % j]
+        te.wait_ge(S["a_d%d" % j], n8)
+        te.matmul(hpd[k][:, 0:ws], w[:, 0:128], T.xs[:, wp:wt], start=True, stop=True).then_inc(S.pe, 1)
+        te.wait_ge(S.ve, 7 + k)
+        mm = te.matmul(T.ys[:, 0:ws], w[:, 128:256], T["hd%d" % k][:, 0:ws], start=False, stop=(k == nch - 1))
+    mm.then_inc(S.pe, 1)
 
     ve.wait_ge(S.fill, 1)
-    for i in range(3):
-        ve.wait_ge(S.pe, i + 1)
-        ve.tensor_tensor(hs[i][:, 0:wt], hp[i][:, 0:wt], T.zero[:, 0:wt], op=AluOpType.max).then_inc(S.ve, 1)
-    ve.wait_ge(S.pe, 4)
-    ve.tensor_tensor(T.h3[:, 0:wp], T.hp3[:, 0:wp], T.zero[:, 0:wp], op=AluOpType.max).then_inc(S.ve, 1)
-    ve.wait_ge(S.pe, 6)
-    ve.tensor_copy(T.pout[:, 0:wp], T.yp[:, 0:wp]).then_inc(S.ve, 1)
-    ve.tensor_tensor(T.h3[:, wp:wt], T.hp4[:, 0:ws], T.zero[:, 0:ws], op=AluOpType.max).then_inc(S.ve, 1)
-    ve.wait_ge(S.pe, 7)
+    ve.wait_ge(S.pe, 1)
+    ve.tensor_tensor(T.h0[:, 0:wt], T.hp0[:, 0:wt], T.zero[:, 0:wt], op=relu).then_inc(S.ve, 1)
+    ve.wait_ge(S.pe, 2)
+    ve.tensor_tensor(T.h1[:, 0:wt], T.hp1[:, 0:wt], T.zero[:, 0:wt], op=relu).then_inc(S.ve, 1)
+    ve.wait_ge(S.pe, 3)
+    ve.tensor_tensor(T.h2[:, 0:wp], T.hp2[:, 0:wp], T.zero[:, 0:wp], op=relu).then_inc(S.ve, 1)
+    ve.wait_ge(S.pe, 5)
+    ve.tensor_copy(T.pout[:, 0:w0], T.yp[:, 0:w0]).then_inc(S.ve, 1)
+    ve.tensor_copy(T.pout[:, w0:wp], T.yp[:, w0:wp]).then_inc(S.ve, 1)
+    ve.tensor_tensor(T.h2[:, wp:wt], T.hp3[:, 0:ws], T.zero[:, 0:ws], op=relu).then_inc(S.ve, 1)
+    for k in range(nch):
+        ve.wait_ge(S.pe, 6 + k)
+        ve.tensor_tensor(T["hd%d" % k][:, 0:ws], hpd[k][:, 0:ws], T.zero[:, 0:ws], op=relu).then_inc(S.ve, 1)
+    ve.wait_ge(S.pe, 9)
     ve.wait_ge(S.a_p0, n8)
     ve.tensor_tensor(T.t1[:, 0:ws], T.ys[:, 0:ws], T.pin0[:, 0:ws], op=AluOpType.add).then_inc(S.ve, 1)
-    ve.wait_ge(S.ve, 7)
+    ve.wait_ge(S.ve, 10)
     ve.wait_ge(S.a_p1, n8)
     ve.tensor_tensor(T.ysb[:, 0:ws], T.t1[:, 0:ws], T.pin1[:, 0:ws], op=AluOpType.add).then_inc(S.ve, 1)
 
-    g.sync.wait_ge(S.ve, 8)
+    g.sync.wait_ge(S.ve, 11)
     g.sync.dma_start(T.y[:, 0:ws], T.ysb[:, 0:ws]).then_inc(S.st, 16)
     g.sync.wait_ge(S.st, 16)

@@ -11,31 +11,43 @@ SCRATCH = {
     "w_d0": ("sbuf", [128, 256], "bfloat16"),
     "w_d1": ("sbuf", [128, 256], "bfloat16"),
     "w_d2": ("sbuf", [128, 256], "bfloat16"),
-    "h0": ("sbuf", [128, XW], "bfloat16"),
-    "h1": ("sbuf", [128, XW], "bfloat16"),
-    "h2": ("sbuf", [128, XW], "bfloat16"),
+    "hv0": ("sbuf", [128, 256], "bfloat16"),
+    "hv1": ("sbuf", [128, 256], "bfloat16"),
+    "hv2": ("sbuf", [128, 256], "bfloat16"),
+    "ho0": ("sbuf", [128, 128], "bfloat16"),
+    "ho1": ("sbuf", [128, 256], "bfloat16"),
     "hd0": ("sbuf", [128, 128], "bfloat16"),
     "hd1": ("sbuf", [128, 128], "bfloat16"),
     "hd2": ("sbuf", [128, 128], "bfloat16"),
-    "zero": ("sbuf", [128, XW], "bfloat16"),
+    "zero": ("sbuf", [128, 256], "bfloat16"),
     "pout": ("sbuf", [128, 256], "bfloat16"),
     "pin0": ("sbuf", [128, 128], "bfloat16"),
     "pin1": ("sbuf", [128, 128], "bfloat16"),
     "ysb": ("sbuf", [128, 128], "bfloat16"),
-    "hp0": ("psum", [128, 512], "float32"),
-    "hp1": ("psum", [128, 512], "float32"),
-    "hp2": ("psum", [128, 512], "float32"),
-    "hp3": ("psum", [128, 512], "float32"),
+    "a0": ("psum", [128, 512], "float32"),
+    "a1": ("psum", [128, 512], "float32"),
+    "b0": ("psum", [128, 512], "float32"),
+    "b1": ("psum", [128, 512], "float32"),
+    "d0": ("psum", [128, 512], "float32"),
+    "d1": ("psum", [128, 512], "float32"),
     "yp": ("psum", [128, 512], "float32"),
     "ys": ("psum", [128, 512], "float32"),
-    "t1": ("psum", [128, 512], "float32"),
 }
-SEMAPHORES = ["ldw", "ldx", "sent", "a_far", "a_near", "a_d0", "a_d1", "a_d2", "a_x", "a_p0", "a_p1", "fill", "pe",
-              "ve", "st"]
+for _w in (16, 32, 48, 80, 112, 128):
+    SCRATCH["xo_%d" % _w] = ("dram", [128, _w], "bfloat16")
+    SCRATCH["xa_%d" % _w] = ("dram", [128, _w], "bfloat16")
+    SCRATCH["xb_%d" % _w] = ("dram", [128, _w], "bfloat16")
+SEMAPHORES = ["ldw", "ldx", "ldd", "lv", "sent", "a_far", "a_fr2", "a_near", "a_d0", "a_d1", "a_d2", "a_e0", "a_e1",
+              "a_e2", "a_xa", "a_xb", "a_p0", "a_p1", "fill", "pe", "ve", "st"]
 
 
 def _engines(mask):
     return bin(mask).count("1")
+
+
+def _half(mask, which):
+    bits = [i for i in range(mask.bit_length()) if (mask >> i) & 1]
+    return sum(1 << i for i in bits[which::2])
 
 
 def _row(c, cores, topo):
@@ -68,102 +80,136 @@ def rank_program(g, core, T, topo):
     place = chips.index(topo.chip(core))
     nch = len(chips)
 
-    def offset(holder, src):
-        o = 0
-        for d in _visitors(holder, cores, topo):
-            if d == src:
-                return o
-            o += wid[d]
+    def slot(holder, src):
+        return "ab"[_visitors(holder, cores, topo).index(src)]
 
     v0, v1 = _visitors(core, cores, topo)
     w0, wp, ws = wid[v0], wid[v0] + wid[v1], wid[core]
     wt = wp + ws
     sent = [0]
+    first = _half(topo.mask(core, v0) & topo.mask(core, v1), 0)
+    n4, n2 = _engines(first), _engines(_half(first, 0))
 
-    def write(dsts, out_aps, in_ap, sem):
+    def fused(parts):
+        trs = []
+        for dsts, out_aps, in_ap, sem, m in parts:
+            ids = [topo.addr(d, core) for d in dsts]
+            trs.append(RemoteDMATransfer(dst_ids=[DstId(rid=r, pnc=p) for r, p in ids], dma_engine_mask=m,
+                                         remote_sem=sem, srcs=[in_ap], dsts=out_aps, alu_op=0))
+            sent[0] += _engines(m)
+        g.remote_dma_fused(trs, local_sem=S.sent)
+
+    def write(dsts, out_aps, in_ap, sem, half=None):
         m = topo.mask(core, dsts[0])
         for d in dsts:
             m &= topo.mask(core, d)
-        ids = [topo.addr(d, core) for d in dsts]
-        g.remote_dma_fused([RemoteDMATransfer(
-            dst_ids=[DstId(rid=r, pnc=p) for r, p in ids], dma_engine_mask=m, remote_sem=sem,
-            srcs=[in_ap], dsts=out_aps, alu_op=0)], local_sem=S.sent)
-        sent[0] += _engines(m)
+        if half is not None:
+            m = _half(m, half)
+        fused([(dsts, out_aps, in_ap, sem, m)])
         return _engines(m)
 
-    g.sync.dma_start(T.w_own[:, 0:128], T.w1[:, :]).then_inc(S.ldw, 16)
-    g.scalar.dma_start(T.w_own[:, 128:256], T.w2[:, :]).then_inc(S.ldw, 16)
-    g.sync.dma_start(T.xs[:, wp:wt], T.x[:, 0:ws]).then_inc(S.ldx, 16)
-    ve.memset(T.zero[:, 0:wt], 0.0).then_inc(S.fill, 1)
+    xdr = T["xo_%d" % ws]
+    g.sync.dma_start(xdr[:, :], T.x[:, 0:ws]).then_inc(S.ldd, 16)
+    g.scalar.dma_start(T.w_own[:, 0:128], T.w1[:, :]).then_inc(S.ldw, 16)
+    g.sync.dma_start(T.w_own[:, 128:256], T.w2[:, :]).then_inc(S.ldw, 16)
+    g.scalar.dma_start(T.xs[:, wp:wt], T.x[:, 0:ws]).then_inc(S.ldx, 16)
+    g.sync.wait_ge(S.a_xa, n2)
+    g.sync.dma_start(T.xs[:, 0:w0], T["xa_%d" % w0][:, :]).then_inc(S.lv, 16)
+    g.scalar.wait_ge(S.a_xb, n2)
+    g.scalar.dma_start(T.xs[:, w0:wp], T["xb_%d" % (wp - w0)][:, :]).then_inc(S.lv, 16)
+    ve.memset(T.zero[:, :], 0.0).then_inc(S.fill, 1)
 
+    g.wait_ge(S.ldd, 16)
+    fused([([d], [T["x%s_%d" % (slot(d, core), ws)][:, :]], xdr[:, :], S["a_x%s" % slot(d, core)], _half(first, k))
+           for k, d in enumerate((v0, v1))])
     g.wait_ge(S.ldw, 32)
-    n8 = write([far], [T.w_far[:]], T.w_own[:], S.a_far)
-    g.wait_ge(S.ldx, 16)
-    write([v0, v1], [T.xs[:, offset(d, core):offset(d, core) + ws] for d in (v0, v1)], T.xs[:, wp:wt], S.a_x)
-    write([near], [T.w_near[:]], T.w_own[:], S.a_near)
+    write([far], [T.w_far[:, 0:128]], T.w_own[:, 0:128], S.a_far, 1)
+    write([far], [T.w_far[:, 128:256]], T.w_own[:, 128:256], S.a_fr2, 1)
+    write([near], [T.w_near[:]], T.w_own[:], S.a_near, 0)
     there = [near] + _row(core, cores, topo)[:-1]
-    g.wait_ge(S.a_far, n8)
-    write(there, [T["w_d%d" % place][:] for d in there], T.w_far[:], S["a_d%d" % place])
-    g.wait_ge(S.ve, 4)
-    write([v0], [T.pin0[:, 0:w0]], T.pout[:, 0:w0], S.a_p0)
+    wdp = T["w_d%d" % place]
+    g.wait_ge(S.a_far, n4)
+    n8 = write(there, [wdp[:, 0:128] for d in there], T.w_far[:, 0:128], S["a_d%d" % place])
+    g.wait_ge(S.a_fr2, n4)
+    write(there, [wdp[:, 128:256] for d in there], T.w_far[:, 128:256], S["a_e%d" % place])
     g.wait_ge(S.ve, 5)
+    write([v0], [T.pin0[:, 0:w0]], T.pout[:, 0:w0], S.a_p0)
+    g.wait_ge(S.ve, 6)
     write([v1], [T.pin1[:, 0:wp - w0]], T.pout[:, w0:wp], S.a_p1)
     g.wait_ge(S.sent, sent[0])
 
-    relu = AluOpType.max
+    xv, xo = T.xs[:, 0:wp], T.xs[:, wp:wt]
+    order = [(place - k) % nch for k in range(nch)]
+    wd = [T["w_d%d" % j] for j in order]
+    ad = [S["a_d%d" % j] for j in order]
+    ae = [S["a_e%d" % j] for j in order]
+    hd = [T.hd0, T.hd1, T.hd2]
+    bd = [T.d0, T.d1, T.d0]
+
     te.wait_ge(S.ldw, 32)
     te.wait_ge(S.ldx, 16)
-    te.wait_ge(S.a_x, 2 * n8)
-    w = T.w_own
-    te.matmul(T.hp0[:, 0:wt], w[:, 0:128], T.xs[:, 0:wt], start=True, stop=True).then_inc(S.pe, 1)
+    te.matmul(T.b0[:, 0:ws], T.w_own[:, 0:128], xo, start=True, stop=True).then_inc(S.pe, 1)
+    te.wait_ge(S.lv, 32)
+    te.matmul(T.a0[:, 0:wp], T.w_own[:, 0:128], xv, start=True, stop=True).then_inc(S.pe, 1)
     te.wait_ge(S.ve, 1)
-    te.matmul(T.yp[:, 0:wp], w[:, 128:256], T.h0[:, 0:wp], start=True, stop=False)
-    te.matmul(T.ys[:, 0:ws], w[:, 128:256], T.h0[:, wp:wt], start=True, stop=False)
-    w = T.w_far
-    te.wait_ge(S.a_far, n8)
-    te.matmul(T.hp1[:, 0:wt], w[:, 0:128], T.xs[:, 0:wt], start=True, stop=True).then_inc(S.pe, 1)
+    te.matmul(T.ys[:, 0:ws], T.w_own[:, 128:256], T.ho0[:, 0:ws], start=True, stop=False)
+    te.wait_ge(S.a_near, n4)
+    te.matmul(T.a1[:, 0:wp], T.w_near[:, 0:128], xv, start=True, stop=True).then_inc(S.pe, 1)
     te.wait_ge(S.ve, 2)
-    te.matmul(T.yp[:, 0:wp], w[:, 128:256], T.h1[:, 0:wp], start=False, stop=False)
-    te.matmul(T.ys[:, 0:ws], w[:, 128:256], T.h1[:, wp:wt], start=False, stop=False)
-    w = T.w_near
-    te.wait_ge(S.a_near, n8)
-    te.matmul(T.hp2[:, 0:wp], w[:, 0:128], T.xs[:, 0:wp], start=True, stop=True).then_inc(S.pe, 1)
-    te.matmul(T.hp3[:, 0:ws], w[:, 0:128], T.xs[:, wp:wt], start=True, stop=True).then_inc(S.pe, 1)
+    te.matmul(T.yp[:, 0:wp], T.w_own[:, 128:256], T.hv0[:, 0:wp], start=True, stop=False)
+    te.wait_ge(S.a_far, n4)
+    te.matmul(T.a0[:, 0:wp], T.w_far[:, 0:128], xv, start=True, stop=True).then_inc(S.pe, 1)
     te.wait_ge(S.ve, 3)
-    te.matmul(T.yp[:, 0:wp], w[:, 128:256], T.h2[:, 0:wp], start=False, stop=True).then_inc(S.pe, 1)
-    te.wait_ge(S.ve, 6)
-    te.matmul(T.ys[:, 0:ws], w[:, 128:256], T.h2[:, wp:wt], start=False, stop=False)
-    order = [(place - k) % nch for k in range(nch)]
-    hpd = [T.hp0, T.hp1, T.hp2]
-    for k, j in enumerate(order):
-        w = T["w_d%d" % j]
-        te.wait_ge(S["a_d%d" % j], n8)
-        te.matmul(hpd[k][:, 0:ws], w[:, 0:128], T.xs[:, wp:wt], start=True, stop=True).then_inc(S.pe, 1)
-        te.wait_ge(S.ve, 7 + k)
-        mm = te.matmul(T.ys[:, 0:ws], w[:, 128:256], T["hd%d" % k][:, 0:ws], start=False, stop=(k == nch - 1))
-    mm.then_inc(S.pe, 1)
+    te.matmul(T.yp[:, 0:wp], T.w_near[:, 128:256], T.hv1[:, 0:wp], start=False, stop=False)
+    te.wait_ge(S.ve, 4)
+    te.wait_ge(S.a_fr2, n4)
+    te.matmul(T.yp[:, 0:wp], T.w_far[:, 128:256], T.hv2[:, 0:wp], start=False, stop=True).then_inc(S.pe, 1)
+    te.matmul(T.b1[:, 0:ws], T.w_far[:, 0:128], xo, start=True, stop=True).then_inc(S.pe, 1)
+    te.matmul(T.b1[:, ws:2 * ws], T.w_near[:, 0:128], xo, start=True, stop=True).then_inc(S.pe, 1)
+    te.wait_ge(ad[0], n8)
+    te.matmul(bd[0][:, 0:ws], wd[0][:, 0:128], xo, start=True, stop=True).then_inc(S.pe, 1)
+    te.wait_ge(S.ve, 7)
+    te.matmul(T.ys[:, 0:ws], T.w_far[:, 128:256], T.ho1[:, 0:ws], start=False, stop=False)
+    te.matmul(T.ys[:, 0:ws], T.w_near[:, 128:256], T.ho1[:, ws:2 * ws], start=False, stop=False)
+    te.wait_ge(ad[1], n8)
+    te.matmul(bd[1][:, 0:ws], wd[1][:, 0:128], xo, start=True, stop=True).then_inc(S.pe, 1)
+    te.wait_ge(S.ve, 8)
+    te.wait_ge(ad[2], n8)
+    te.matmul(bd[2][:, 0:ws], wd[2][:, 0:128], xo, start=True, stop=True).then_inc(S.pe, 1)
+    te.wait_ge(ae[0], n8)
+    te.matmul(T.ys[:, 0:ws], wd[0][:, 128:256], hd[0][:, 0:ws], start=False, stop=False)
+    te.wait_ge(S.ve, 9)
+    te.wait_ge(ae[1], n8)
+    te.matmul(T.ys[:, 0:ws], wd[1][:, 128:256], hd[1][:, 0:ws], start=False, stop=False)
+    te.wait_ge(S.ve, 10)
+    te.wait_ge(ae[2], n8)
+    te.matmul(T.ys[:, 0:ws], wd[2][:, 128:256], hd[2][:, 0:ws], start=False, stop=True).then_inc(S.pe, 1)
 
+    relu, add = AluOpType.max, AluOpType.add
     ve.wait_ge(S.fill, 1)
     ve.wait_ge(S.pe, 1)
-    ve.tensor_tensor(T.h0[:, 0:wt], T.hp0[:, 0:wt], T.zero[:, 0:wt], op=relu).then_inc(S.ve, 1)
+    ve.tensor_tensor(T.ho0[:, 0:ws], T.b0[:, 0:ws], T.zero[:, 0:ws], op=relu).then_inc(S.ve, 1)
     ve.wait_ge(S.pe, 2)
-    ve.tensor_tensor(T.h1[:, 0:wt], T.hp1[:, 0:wt], T.zero[:, 0:wt], op=relu).then_inc(S.ve, 1)
+    ve.tensor_tensor(T.hv0[:, 0:wp], T.a0[:, 0:wp], T.zero[:, 0:wp], op=relu).then_inc(S.ve, 1)
     ve.wait_ge(S.pe, 3)
-    ve.tensor_tensor(T.h2[:, 0:wp], T.hp2[:, 0:wp], T.zero[:, 0:wp], op=relu).then_inc(S.ve, 1)
+    ve.tensor_tensor(T.hv1[:, 0:wp], T.a1[:, 0:wp], T.zero[:, 0:wp], op=relu).then_inc(S.ve, 1)
+    ve.wait_ge(S.pe, 4)
+    ve.tensor_tensor(T.hv2[:, 0:wp], T.a0[:, 0:wp], T.zero[:, 0:wp], op=relu).then_inc(S.ve, 1)
     ve.wait_ge(S.pe, 5)
     ve.tensor_copy(T.pout[:, 0:w0], T.yp[:, 0:w0]).then_inc(S.ve, 1)
     ve.tensor_copy(T.pout[:, w0:wp], T.yp[:, w0:wp]).then_inc(S.ve, 1)
-    ve.tensor_tensor(T.h2[:, wp:wt], T.hp3[:, 0:ws], T.zero[:, 0:ws], op=relu).then_inc(S.ve, 1)
+    ve.wait_ge(S.pe, 7)
+    ve.tensor_tensor(T.ho1[:, 0:2 * ws], T.b1[:, 0:2 * ws], T.zero[:, 0:2 * ws], op=relu).then_inc(S.ve, 1)
     for k in range(nch):
-        ve.wait_ge(S.pe, 6 + k)
-        ve.tensor_tensor(T["hd%d" % k][:, 0:ws], hpd[k][:, 0:ws], T.zero[:, 0:ws], op=relu).then_inc(S.ve, 1)
-    ve.wait_ge(S.pe, 9)
+        ve.wait_ge(S.pe, 8 + k)
+        ve.tensor_tensor(hd[k][:, 0:ws], bd[k][:, 0:ws], T.zero[:, 0:ws], op=relu).then_inc(S.ve, 1)
+    ve.wait_ge(S.pe, 11)
     ve.wait_ge(S.a_p0, n8)
-    ve.tensor_tensor(T.t1[:, 0:ws], T.ys[:, 0:ws], T.pin0[:, 0:ws], op=AluOpType.add).then_inc(S.ve, 1)
-    ve.wait_ge(S.ve, 10)
+    ve.tensor_tensor(T.b0[:, 0:ws], T.ys[:, 0:ws], T.pin0[:, 0:ws], op=add).then_inc(S.ve, 1)
+    ve.wait_ge(S.ve, 11)
     ve.wait_ge(S.a_p1, n8)
-    ve.tensor_tensor(T.ysb[:, 0:ws], T.t1[:, 0:ws], T.pin1[:, 0:ws], op=AluOpType.add).then_inc(S.ve, 1)
+    ve.tensor_tensor(T.ysb[:, 0:ws], T.b0[:, 0:ws], T.pin1[:, 0:ws], op=add).then_inc(S.ve, 1)
 
-    g.sync.wait_ge(S.ve, 11)
+    g.sync.wait_ge(S.ve, 12)
     g.sync.dma_start(T.y[:, 0:ws], T.ysb[:, 0:ws]).then_inc(S.st, 16)
     g.sync.wait_ge(S.st, 16)

from concourse.bass import DstId, RemoteDMATransfer
from concourse.mybir import AluOpType

XW = 304

SCRATCH = {
    "xs": ("sbuf", [128, XW], "bfloat16"),
    "w_own": ("sbuf", [128, 256], "bfloat16"),
    "w_far": ("sbuf", [128, 256], "bfloat16"),
    "w_near": ("sbuf", [128, 256], "bfloat16"),
    "w_d0": ("sbuf", [128, 256], "bfloat16"),
    "w_d1": ("sbuf", [128, 256], "bfloat16"),
    "w_d2": ("sbuf", [128, 256], "bfloat16"),
    "hv0": ("sbuf", [128, 256], "bfloat16"),
    "hv1": ("sbuf", [128, 256], "bfloat16"),
    "hv2": ("sbuf", [128, 256], "bfloat16"),
    "ho0": ("sbuf", [128, 128], "bfloat16"),
    "ho1": ("sbuf", [128, 256], "bfloat16"),
    "hd0": ("sbuf", [128, 128], "bfloat16"),
    "hd1": ("sbuf", [128, 128], "bfloat16"),
    "hd2": ("sbuf", [128, 128], "bfloat16"),
    "zero": ("sbuf", [128, 256], "bfloat16"),
    "pout": ("sbuf", [128, 256], "bfloat16"),
    "pin0": ("sbuf", [128, 128], "bfloat16"),
    "pin1": ("sbuf", [128, 128], "bfloat16"),
    "ysb": ("sbuf", [128, 128], "bfloat16"),
    "a0": ("psum", [128, 512], "float32"),
    "a1": ("psum", [128, 512], "float32"),
    "b0": ("psum", [128, 512], "float32"),
    "b1": ("psum", [128, 512], "float32"),
    "d0": ("psum", [128, 512], "float32"),
    "d1": ("psum", [128, 512], "float32"),
    "yp": ("psum", [128, 512], "float32"),
    "ys": ("psum", [128, 512], "float32"),
}
for _w in (16, 32, 48, 80, 112, 128):
    SCRATCH["xo_%d" % _w] = ("dram", [128, _w], "bfloat16")
    SCRATCH["xa_%d" % _w] = ("dram", [128, _w], "bfloat16")
    SCRATCH["xb_%d" % _w] = ("dram", [128, _w], "bfloat16")
SEMAPHORES = ["ldw", "ldx", "ldd", "lv", "sent", "a_far", "a_fr2", "a_near", "a_d0", "a_d1", "a_d2", "a_e0", "a_e1",
              "a_e2", "a_xa", "a_xb", "a_p0", "a_p1", "fill", "pe", "ve", "st"]


def _engines(mask):
    return bin(mask).count("1")


def _half(mask, which):
    bits = [i for i in range(mask.bit_length()) if (mask >> i) & 1]
    return sum(1 << i for i in bits[which::2])


def _row(c, cores, topo):
    row = [d for d in cores if topo.host(d) == topo.host(c)]
    i = row.index(c)
    return row[i + 1:] + row[:i] + [c]


def _near(c, cores, topo):
    return [d for d in cores if d != c and topo.chip(d) == topo.chip(c)
            and topo.rack(topo.host(d)) == topo.rack(topo.host(c))][0]


def _visitors(c, cores, topo):
    return _row(_near(c, cores, topo), cores, topo)[:-1]


def rank_program(g, core, T, topo):
    rank = T.rank_of(core)
    if rank is None:
        return
    cores, S = list(T.cores), T.sem
    wid = {d: T.tables["WID"][T.rank_of(d)] for d in cores}
    te, ve = g.tensor, g.vector

    near = _near(core, cores, topo)
    far = [d for d in cores if topo.chip(d) == topo.chip(core) and topo.rack(topo.host(d)) != topo.rack(topo.host(core))
           and topo.may_write(core, d)][0]
    chips = sorted({topo.chip(d) for d in cores})
    place = chips.index(topo.chip(core))
    nch = len(chips)

    def slot(holder, src):
        return "ab"[_visitors(holder, cores, topo).index(src)]

    v0, v1 = _visitors(core, cores, topo)
    w0, wp, ws = wid[v0], wid[v0] + wid[v1], wid[core]
    wt = wp + ws
    sent = [0]
    first = _half(topo.mask(core, v0) & topo.mask(core, v1), 0)
    n4, n2 = _engines(first), _engines(_half(first, 0))

    def fused(parts):
        trs = []
        for dsts, out_aps, in_ap, sem, m in parts:
            ids = [topo.addr(d, core) for d in dsts]
            trs.append(RemoteDMATransfer(dst_ids=[DstId(rid=r, pnc=p) for r, p in ids], dma_engine_mask=m,
                                         remote_sem=sem, srcs=[in_ap], dsts=out_aps, alu_op=0))
            sent[0] += _engines(m)
        g.remote_dma_fused(trs, local_sem=S.sent)

    def write(dsts, out_aps, in_ap, sem, half=None):
        m = topo.mask(core, dsts[0])
        for d in dsts:
            m &= topo.mask(core, d)
        if half is not None:
            m = _half(m, half)
        fused([(dsts, out_aps, in_ap, sem, m)])
        return _engines(m)

    xdr = T["xo_%d" % ws]
    g.sync.dma_start(xdr[:, :], T.x[:, 0:ws]).then_inc(S.ldd, 16)
    g.scalar.dma_start(T.w_own[:, 0:128], T.w1[:, :]).then_inc(S.ldw, 16)
    g.sync.dma_start(T.w_own[:, 128:256], T.w2[:, :]).then_inc(S.ldw, 16)
    g.scalar.dma_start(T.xs[:, wp:wt], T.x[:, 0:ws]).then_inc(S.ldx, 16)
    g.sync.wait_ge(S.a_xa, n2)
    g.sync.dma_start(T.xs[:, 0:w0], T["xa_%d" % w0][:, :]).then_inc(S.lv, 16)
    g.scalar.wait_ge(S.a_xb, n2)
    g.scalar.dma_start(T.xs[:, w0:wp], T["xb_%d" % (wp - w0)][:, :]).then_inc(S.lv, 16)
    ve.memset(T.zero[:, :], 0.0).then_inc(S.fill, 1)

    g.wait_ge(S.ldd, 16)
    fused([([d], [T["x%s_%d" % (slot(d, core), ws)][:, :]], xdr[:, :], S["a_x%s" % slot(d, core)], _half(first, k))
           for k, d in enumerate((v0, v1))])
    g.wait_ge(S.ldw, 32)
    write([far], [T.w_far[:, 0:128]], T.w_own[:, 0:128], S.a_far, 1)
    write([far], [T.w_far[:, 128:256]], T.w_own[:, 128:256], S.a_fr2, 1)
    write([near], [T.w_near[:]], T.w_own[:], S.a_near, 0)
    there = [near] + _row(core, cores, topo)[:-1]
    wdp = T["w_d%d" % place]
    g.wait_ge(S.a_far, n4)
    n8 = write(there, [wdp[:, 0:128] for d in there], T.w_far[:, 0:128], S["a_d%d" % place])
    g.wait_ge(S.a_fr2, n4)
    write(there, [wdp[:, 128:256] for d in there], T.w_far[:, 128:256], S["a_e%d" % place])
    g.wait_ge(S.ve, 5)
    write([v0], [T.pin0[:, 0:w0]], T.pout[:, 0:w0], S.a_p0)
    g.wait_ge(S.ve, 6)
    write([v1], [T.pin1[:, 0:wp - w0]], T.pout[:, w0:wp], S.a_p1)
    g.wait_ge(S.sent, sent[0])

    xv, xo = T.xs[:, 0:wp], T.xs[:, wp:wt]
    order = [(place - k) % nch for k in range(nch)]
    wd = [T["w_d%d" % j] for j in order]
    ad = [S["a_d%d" % j] for j in order]
    ae = [S["a_e%d" % j] for j in order]
    hd = [T.hd0, T.hd1, T.hd2]
    bd = [T.d0, T.d1, T.d0]

    te.wait_ge(S.ldw, 32)
    te.wait_ge(S.ldx, 16)
    te.matmul(T.b0[:, 0:ws], T.w_own[:, 0:128], xo, start=True, stop=True).then_inc(S.pe, 1)
    te.wait_ge(S.lv, 32)
    te.matmul(T.a0[:, 0:wp], T.w_own[:, 0:128], xv, start=True, stop=True).then_inc(S.pe, 1)
    te.wait_ge(S.ve, 1)
    te.matmul(T.ys[:, 0:ws], T.w_own[:, 128:256], T.ho0[:, 0:ws], start=True, stop=False)
    te.wait_ge(S.a_near, n4)
    te.matmul(T.a1[:, 0:wp], T.w_near[:, 0:128], xv, start=True, stop=True).then_inc(S.pe, 1)
    te.wait_ge(S.ve, 2)
    te.matmul(T.yp[:, 0:wp], T.w_own[:, 128:256], T.hv0[:, 0:wp], start=True, stop=False)
    te.wait_ge(S.a_far, n4)
    te.matmul(T.a0[:, 0:wp], T.w_far[:, 0:128], xv, start=True, stop=True).then_inc(S.pe, 1)
    te.wait_ge(S.ve, 3)
    te.matmul(T.yp[:, 0:wp], T.w_near[:, 128:256], T.hv1[:, 0:wp], start=False, stop=False)
    te.wait_ge(S.ve, 4)
    te.wait_ge(S.a_fr2, n4)
    te.matmul(T.yp[:, 0:wp], T.w_far[:, 128:256], T.hv2[:, 0:wp], start=False, stop=True).then_inc(S.pe, 1)
    te.matmul(T.b1[:, 0:ws], T.w_far[:, 0:128], xo, start=True, stop=True).then_inc(S.pe, 1)
    te.matmul(T.b1[:, ws:2 * ws], T.w_near[:, 0:128], xo, start=True, stop=True).then_inc(S.pe, 1)
    te.wait_ge(ad[0], n8)
    te.matmul(bd[0][:, 0:ws], wd[0][:, 0:128], xo, start=True, stop=True).then_inc(S.pe, 1)
    te.wait_ge(S.ve, 7)
    te.matmul(T.ys[:, 0:ws], T.w_far[:, 128:256], T.ho1[:, 0:ws], start=False, stop=False)
    te.matmul(T.ys[:, 0:ws], T.w_near[:, 128:256], T.ho1[:, ws:2 * ws], start=False, stop=False)
    te.wait_ge(ad[1], n8)
    te.matmul(bd[1][:, 0:ws], wd[1][:, 0:128], xo, start=True, stop=True).then_inc(S.pe, 1)
    te.wait_ge(S.ve, 8)
    te.wait_ge(ad[2], n8)
    te.matmul(bd[2][:, 0:ws], wd[2][:, 0:128], xo, start=True, stop=True).then_inc(S.pe, 1)
    te.wait_ge(ae[0], n8)
    te.matmul(T.ys[:, 0:ws], wd[0][:, 128:256], hd[0][:, 0:ws], start=False, stop=False)
    te.wait_ge(S.ve, 9)
    te.wait_ge(ae[1], n8)
    te.matmul(T.ys[:, 0:ws], wd[1][:, 128:256], hd[1][:, 0:ws], start=False, stop=False)
    te.wait_ge(S.ve, 10)
    te.wait_ge(ae[2], n8)
    te.matmul(T.ys[:, 0:ws], wd[2][:, 128:256], hd[2][:, 0:ws], start=False, stop=True).then_inc(S.pe, 1)

    relu, add = AluOpType.max, AluOpType.add
    ve.wait_ge(S.fill, 1)
    ve.wait_ge(S.pe, 1)
    ve.tensor_tensor(T.ho0[:, 0:ws], T.b0[:, 0:ws], T.zero[:, 0:ws], op=relu).then_inc(S.ve, 1)
    ve.wait_ge(S.pe, 2)
    ve.tensor_tensor(T.hv0[:, 0:wp], T.a0[:, 0:wp], T.zero[:, 0:wp], op=relu).then_inc(S.ve, 1)
    ve.wait_ge(S.pe, 3)
    ve.tensor_tensor(T.hv1[:, 0:wp], T.a1[:, 0:wp], T.zero[:, 0:wp], op=relu).then_inc(S.ve, 1)
    ve.wait_ge(S.pe, 4)
    ve.tensor_tensor(T.hv2[:, 0:wp], T.a0[:, 0:wp], T.zero[:, 0:wp], op=relu).then_inc(S.ve, 1)
    ve.wait_ge(S.pe, 5)
    ve.tensor_copy(T.pout[:, 0:w0], T.yp[:, 0:w0]).then_inc(S.ve, 1)
    ve.tensor_copy(T.pout[:, w0:wp], T.yp[:, w0:wp]).then_inc(S.ve, 1)
    ve.wait_ge(S.pe, 7)
    ve.tensor_tensor(T.ho1[:, 0:2 * ws], T.b1[:, 0:2 * ws], T.zero[:, 0:2 * ws], op=relu).then_inc(S.ve, 1)
    for k in range(nch):
        ve.wait_ge(S.pe, 8 + k)
        ve.tensor_tensor(hd[k][:, 0:ws], bd[k][:, 0:ws], T.zero[:, 0:ws], op=relu).then_inc(S.ve, 1)
    ve.wait_ge(S.pe, 11)
    ve.wait_ge(S.a_p0, n8)
    ve.tensor_tensor(T.b0[:, 0:ws], T.ys[:, 0:ws], T.pin0[:, 0:ws], op=add).then_inc(S.ve, 1)
    ve.wait_ge(S.ve, 11)
    ve.wait_ge(S.a_p1, n8)
    ve.tensor_tensor(T.ysb[:, 0:ws], T.b0[:, 0:ws], T.pin1[:, 0:ws], op=add).then_inc(S.ve, 1)

    g.sync.wait_ge(S.ve, 12)
    g.sync.dma_start(T.y[:, 0:ws], T.ysb[:, 0:ws]).then_inc(S.st, 16)
    g.sync.wait_ge(S.st, 16)
